import numpy as np
import ml_dtypes


def mxq(x, axis, fmt="e4m3"):
    dtype, down = {"e4m3": (ml_dtypes.float8_e4m3fn, 7), "e5m2": (ml_dtypes.float8_e5m2, 14)}[fmt]
    v = np.moveaxis(np.asarray(x, np.float32).astype(ml_dtypes.bfloat16).astype(np.float64), axis, -1)
    blocks = v.reshape(v.shape[:-1] + (-1, 32))
    amax = np.abs(blocks).max(-1, keepdims=True)
    byte = np.maximum(np.where(amax > 0, np.frexp(amax)[1] - 1 + 127, 0) - down, 1)
    scale = np.exp2(byte - 127.0)
    codes = (blocks / scale).astype(np.float32).astype(dtype).astype(np.float64)
    return np.moveaxis((codes * scale).reshape(v.shape), -1, axis)


WIDE = False


def mx_kscale(k):
    if not WIDE:
        return np.ones(k)
    levels = np.array([30, -30])
    if k % 512:
        return np.exp2(np.random.permutation(np.resize(levels, k // 32))).repeat(32)
    a = np.empty((k // 512, 16))
    for p in range(k // 512):
        a[p, :8] = np.random.permutation(np.resize(levels, 8))
        for g in range(8):
            far = levels[np.abs(levels - a[p, g]) >= 10]
            a[p, g + 8] = far[np.random.randint(len(far))]
    return np.exp2(a.ravel()).repeat(32)


BF16 = ml_dtypes.bfloat16


def bf(x):
    return np.asarray(x, np.float32).astype(BF16)


def f64(x):
    return np.asarray(x).astype(np.float64)


P, T, V, D = 1024, 2048, 1536, 1024


def setup_inputs():
    s, t = mx_kscale(P), mx_kscale(T)
    heavy = np.exp(np.random.standard_normal((T, D))) / np.e
    return {"logits": bf(np.random.standard_normal((P, V))),
            "target": bf(np.random.random((P, V))),
            "lossw": bf((0.5 + np.random.random(P)) * 3.0 / np.sqrt(P) * s),
            "hid": bf(np.random.standard_normal((P, D)) / s[:, None]),
            "codes": bf(np.random.standard_normal((T, V)) * t[:, None]),
            "dx": bf(np.random.standard_normal((T, D)) * heavy / np.sqrt(T) / t[:, None]),
            "table": bf(0.3 * np.random.standard_normal((V, D))),
            "step": bf(0.5 + np.random.random(V))}


def reference(logits, target, lossw, hid, codes, dx, table, step):
    prob = 1.0 / (1.0 + np.exp(-f64(logits)))
    res = (prob - f64(target)) * f64(lossw)[:, None]
    head = mxq(res, 0, "e4m3").T @ mxq(f64(hid), 0, "e4m3")
    emb = mxq(f64(codes), 0, "e4m3").T @ mxq(f64(dx), 0, "e5m2")
    grad = head + emb
    return f64(table) - f64(step)[:, None] * grad

from contextlib import ExitStack

import concourse.mybir as mybir
from concourse.masks import make_identity

F32 = mybir.dt.float32
BF16 = mybir.dt.bfloat16
U32 = mybir.dt.uint32
U8 = mybir.dt.uint8
E4M3 = mybir.dt.float8_e4m3fn_x4
E5M2 = mybir.dt.float8_e5m2_x4
ALU = mybir.AluOpType
SIGMOID = mybir.ActivationFunctionType.Sigmoid

POS, TOK, VOC, DIM = 1024, 2048, 1536, 1024
FLOPS = 2 * (POS + TOK) * VOC * DIM

K_PASS = 512
HALF = 512
GROUPS = ((0, 256), (256, 256), (512, 256), (768, 256), (1024, 256), (1280, 256))
JOBS = ((0, (0, 1), 0), (1, (0, 1), 4), (2, (0, 1), 0), (3, (0, 1), 4), (4, (0, 1), 0), (5, (0, 1), 4))
CODE_BLOCKS = (((0, 512), (512, 512), (1024, 512)), ((0, 512), (512, 512), (1024, 512)), ((0, 512), (512, 512), (1024, 512)), ((0, 512), (512, 512), (1024, 512)))
HEAD_BLOCKS = (((0, 512), (512, 512), (1024, 512)), ((0, 512), (512, 512), (1024, 512)))

LOADS = (
    "Lg10", "Lt10", "Lc10", "Lx2", "Lg01", "Lt01", "Lc30", "Lh1", "Lc20", "Lx3", "Lh0", "Lx1",
    "Lg00", "Lt00", "Lx0", "Lg11", "Lc00", "Lt11", "T0", "Lc31", "Lc21", "Lc11", "Lg12", "Lc01",
    "Lt12", "Lg02", "Lt02", "Lc32", "T1", "Lc12", "w10", "Lc22", "Lc02", "w11", "T2", "w01", "w21",
    "w31", "w20", "w00", "w30", "w50", "w51", "w40", "w41",
)
SCALAR = (
    "sR10", "sR11", "iC10", "iC11", "iX21", "sR03", "sR02", "iC31", "iC30", "iH10", "iC21", "iC20",
    "iX31", "iH01", "iX11", "sR00", "sR01", "iX00", "iX01", "sR13", "iC01", "iC00", "sR12", "iC33",
    "iC23", "iC22", "iC13", "sR15", "iC32", "iC02", "sR05", "iC12", "iC03", "iC35", "sR04", "sR14",
    "iC15", "iC34", "iC14", "iC25", "iC05", "iC04", "iC24",
)
VECTOR = (
    "bR10", "bR11", "mR10", "mR11", "iX20", "qC10", "qR11", "qX20", "qX21", "qR10", "bR03", "bR02",
    "mR03", "iH11", "qC11", "qH11", "qC31", "qR03", "mR02", "qC30", "iX30", "qC20", "qR02", "qC21",
    "iH00", "qH10", "qX31", "iX10", "qX30", "qH00", "qH01", "qX11", "qX10", "bR00", "bR01", "mR00",
    "mR01", "qX00", "qR00", "qX01", "qR01", "bR13", "qC01", "mR13", "e101", "qC00", "e110", "e100",
    "qR13", "e111", "qC33", "e011", "e000", "qC23", "e001", "e010", "qC22", "bR12", "qC13", "bR15",
    "mR12", "mR15", "qC02", "qC32", "bR05", "qC03", "qC12", "mR05", "qR15", "qR12", "e300", "e301",
    "e311", "e310", "qC15", "e211", "qC35", "qR05", "e210", "qC34", "bR14", "qC25", "e201", "qC05",
    "e200", "mR14", "qC14", "e501", "qC24", "qR14", "bR04", "qC04", "e500", "mR04", "qR04", "e511",
    "e510", "e401", "e400", "e411", "e410",
)


def tile_tied_code_head_step_s2_kernel(tc, logits, target, lossw, hid, codes, dx, table, step, out):
    nc = tc.nc
    with ExitStack() as ctx:
        raw = ctx.enter_context(tc.tile_pool(name="raw", bufs=3))
        work = ctx.enter_context(tc.tile_pool(name="work", bufs=3))
        keep = ctx.enter_context(tc.tile_pool(name="keep", bufs=1))
        psum = ctx.enter_context(tc.psum_pool(name="psum", bufs=1))

        lw = keep.tile([128, 2, 4], BF16, name="lw")
        st_rows = keep.tile([128, 128], BF16, name="st_rows", align_bytes=64)
        ident = keep.tile([128, 128], BF16, name="ident", align_bytes=64)
        warm = keep.tile([128, 1], F32, name="warm")
        neg_step = keep.tile([128, 12], F32, name="neg_step")

        ctx.enter_context(tc.manual_schedule())
        nc.gpsimd.memset(warm[:], 0.0)
        nc.gpsimd.memset(st_rows[:], 0.0)
        make_identity(nc, ident[:])
        nc.scalar.activation(out=warm[:], in_=warm[:], func=SIGMOID)
        nc.scalar.dma_start(out=lw[:], in_=lossw.rearrange("(c p j) -> p c j", c=2, j=4))
        nc.scalar.dma_start(out=st_rows[0:12, :], in_=step.rearrange("(t p) -> t p", p=128))
        st_cols = psum.tile([128, 128], BF16, name="acc7", tag="acc7")
        nc.tensor.transpose(st_cols[:], st_rows[:], ident[:])

        loaded = {}
        interleaved = {}
        prob = {}
        codes_of = {}
        scales_of = {}
        acc = {}
        result = {}
        stepped = set()
        bufs = {512: 12, 1024: 5}
        widest = max(width for first, width in GROUPS)

        def raw_tile(columns):
            nm = "raw%d" % columns
            return raw.tile([128, 4, columns], BF16, name=nm, tag=nm, bufs=bufs[columns])

        def issue(key):
            if key[0] == "w":
                j, v = int(key[1]), int(key[2])
                halves = JOBS[j][1]
                row = GROUPS[JOBS[j][0]][0] + 128 * v
                first = HALF * (int(key[3]) if len(halves) == 1 else 0)
                nc.sync.dma_start(out=out[row:row + 128, first:first + HALF * len(halves)], in_=result[key[1:]][:])
                return
            if key[0] == "T":
                b = int(key[1])
                t = raw_tile(DIM)
                nc.sync.dma_start(out=t[:], in_=table[b * 512:(b + 1) * 512, :].rearrange("(t p) d -> p t d", p=128))
                loaded[key] = t
                return
            kind, c = key[1], int(key[2])
            src = {"x": dx, "h": hid, "c": codes, "g": logits, "t": target}[kind]
            if kind in "xh":
                first, width = 0, DIM
            else:
                first, width = (CODE_BLOCKS if kind == "c" else HEAD_BLOCKS)[c][int(key[3])]
            t = raw_tile(width)
            nc.sync.dma_start(
                out=t[:],
                in_=src[c * K_PASS:(c + 1) * K_PASS, first:first + width].rearrange("(p j) w -> p j w", j=4),
            )
            loaded[key] = t

        issued = [0]

        def need(key):
            while key not in loaded:
                issue(LOADS[issued[0]])
                issued[0] += 1

        def parts(u):
            kind, c = u[0], u[1]
            if kind in "XH":
                h = int(u[2])
                return ["L" + {"X": "x", "H": "h"}[kind] + c], slice(h * HALF, (h + 1) * HALF), HALF
            first, width = GROUPS[int(u[2])]
            blocks = (CODE_BLOCKS if kind == "C" else HEAD_BLOCKS)[int(c)]
            b = [i for i, (f, w) in enumerate(blocks) if f <= first and first + width <= f + w][0]
            cols = slice(first - blocks[b][0], first - blocks[b][0] + width)
            b = c + str(b)
            return ["Lc" + b] if kind == "C" else ["Lg" + b, "Lt" + b], cols, width

        def scalar_op(x):
            u = x[1:]
            keys, cols, width = parts(u)
            need(keys[0])
            src = loaded[keys[0]][:, :, cols]
            if x[0] == "s":
                t = work.tile([128, 4 * widest], F32, name="prob", tag="prob", bufs=3)
                nc.scalar.activation(out=t[:, :4 * width].rearrange("p (j w) -> p j w", j=4), in_=src, func=SIGMOID)
                prob[u] = t
                return
            t = work.tile([128, 2048], BF16, name="xs", tag="xs", bufs=5, align_bytes=64)
            nc.scalar.copy(
                out=t[:, :4 * width].rearrange("p (c i j) -> p c j i", i=4, j=4),
                in_=src.rearrange("p j (c i) -> p c j i", i=4),
            )
            interleaved[u] = t

        done = [0]

        def scalar_until(x):
            while x not in SCALAR[:done[0]]:
                scalar_op(SCALAR[done[0]])
                done[0] += 1

        def vector_op(x):
            k, u = x[0], x[1:]
            if k == "e":
                j, v, h = int(u[0]), int(u[1]), int(u[2])
                tile_no = GROUPS[JOBS[j][0]][0] // 128 + v
                tab = "T" + str(tile_no // 4)
                need(tab)
                halves = JOBS[j][1]
                dest = u if len(halves) == 1 else u[:2]
                if dest not in result:
                    result[dest] = work.tile([128, HALF * len(halves)], F32, name="o", tag="o", bufs=6)
                at = HALF * halves.index(h)
                nc.vector.scalar_tensor_tensor(
                    out=result[dest][:, at:at + HALF],
                    in0=acc[(j, v, h)][:],
                    scalar=neg_step[:, tile_no:tile_no + 1],
                    in1=loaded[tab][:, tile_no % 4, h * HALF:(h + 1) * HALF],
                    op0=ALU.mult,
                    op1=ALU.add,
                )
                stepped.add((j, v, h))
                return
            keys, cols, width = parts(u)
            if k == "i":
                need(keys[0])
                t = work.tile([128, 2048], BF16, name="xv", tag="xv", bufs=3, align_bytes=64)
                nc.vector.tensor_copy(
                    out=t[:, :4 * width].rearrange("p (c i j) -> p c j i", i=4, j=4),
                    in_=loaded[keys[0]][:, :, cols].rearrange("p j (c i) -> p c j i", i=4),
                )
                interleaved[u] = t
            elif k == "b":
                scalar_until("s" + u)
                need(keys[1])
                p = prob[u][:, :4 * width].rearrange("p (j w) -> p j w", j=4)
                nc.vector.tensor_tensor(out=p, in0=p, in1=loaded[keys[1]][:, :, cols], op=ALU.subtract)
            elif k == "m":
                t = work.tile([128, 2048], BF16, name="xv", tag="xv", bufs=3, align_bytes=64)
                nc.vector.tensor_tensor(
                    out=t[:, :4 * width].rearrange("p (c i j) -> p c j i", i=4, j=4),
                    in0=prob[u][:, :4 * width].rearrange("p (j c i) -> p c j i", j=4, i=4),
                    in1=lw[:, int(u[1]), :].unsqueeze(1).unsqueeze(3).to_broadcast([128, width // 4, 4, 4]),
                    op=ALU.mult,
                )
                interleaved[u] = t
            else:
                if "i" + u in SCALAR:
                    scalar_until("i" + u)
                cw = keep.tile([128, width], U32, name="w" + u, align_bytes=64)
                cs = keep.tile([128, width], U8, name="s" + u, align_bytes=64)
                nc.vector.quantize_mx(
                    out=cw[:].bitcast(E5M2 if u[0] == "X" else E4M3),
                    scales=cs[:],
                    in_=interleaved[u][:, :4 * width],
                )
                codes_of[u] = cw
                scales_of[u] = cs

        def multiply(j, u, v, first, last):
            g, halves, bank = JOBS[j]
            vs = slice(v * 128, (v + 1) * 128)
            for i, h in enumerate(halves):
                r = ("X" if u[0] == "C" else "H") + u[1] + str(h)
                if first:
                    nm = "acc" + str(bank + v * len(halves) + i)
                    acc[(j, v, h)] = psum.tile([128, HALF], F32, name=nm, tag=nm)
                nc.tensor.matmul_mx(
                    out=acc[(j, v, h)][:],
                    lhsT=codes_of[u][:, vs].bitcast(E4M3),
                    lhsT_scale=scales_of[u][:, vs],
                    rhs=codes_of[r][:].bitcast(E5M2 if r[0] == "X" else E4M3),
                    rhs_scale=scales_of[r][:],
                    start=first,
                    stop=last,
                )

        quantized = [x[1:] for x in VECTOR if x[0] == "q"]
        waiting = [[u for u in quantized if u[0] in "CR" and int(u[2]) == g] for g, halves, bank in JOBS]
        users = {}
        for j, (g, halves, bank) in enumerate(JOBS):
            for v in range(GROUPS[g][1] // 128):
                for i, h in enumerate(halves):
                    users.setdefault(bank + v * len(halves) + i, []).append((j, v, h))

        def free(j):
            for seq in users.values():
                for k, (jj, v, h) in enumerate(seq):
                    if jj == j and k > 0 and seq[k - 1] not in stepped:
                        return False
            return True

        def passes():
            again = True
            while again:
                again = False
                for j, (g, halves, bank) in enumerate(JOBS):
                    first = len(waiting[j]) == 6
                    if again or not waiting[j] or (first and not free(j)):
                        continue
                    ok = [
                        u for u in waiting[j]
                        if u in codes_of and all(("X" if u[0] == "C" else "H") + u[1] + str(h) in codes_of for h in halves)
                    ]
                    if ok:
                        waiting[j].remove(ok[0])
                        for v in range(GROUPS[g][1] // 128):
                            multiply(j, ok[0], v, first, not waiting[j])
                        again = True

        for i, x in enumerate(VECTOR):
            vector_op(x)
            if i == 4:
                nc.vector.tensor_scalar(out=neg_step[:], in0=st_cols[:, 0:12], scalar1=-1.0, scalar2=None, op0=ALU.mult)
            passes()
        for x in LOADS[issued[0]:]:
            issue(x)
